import numpy as np
import ml_dtypes

BF16 = ml_dtypes.bfloat16


def bf(x):
    return np.asarray(x, np.float32).astype(BF16)


def f32(x):
    return np.asarray(x, np.float32)


def f64(x):
    return np.asarray(x).astype(np.float64)


def striped(idx):
    return np.tile(idx.reshape(-1, 16).T, (8, 1))


def rows(idx, k):
    return np.tile(idx, (k, 1))


def look(tab, idx):
    return np.take_along_axis(f64(tab), rows(idx, len(tab)), axis=1)


K, S, V, N, M = 256, 2048, 2048, 2048, 128


def silu(v):
    return v / (1.0 + np.exp(-v))


def setup_inputs():
    return {"tab": f32(np.random.standard_normal((2, K, S))), "y": f32(np.random.standard_normal((K, V))), "w": bf(np.random.standard_normal((K, M)) / np.sqrt(K)), "b": f32(0.5 * np.random.standard_normal((M, 1))), "offs": striped(np.random.permutation(S)[:N])}


def reference(tab, y, w, b, offs):
    idx = offs[:16].T.reshape(-1)
    x = (np.maximum(look(tab[0], idx), f64(y))) * (silu(look(tab[1], idx)))
    return np.maximum(f64(w).T @ x + f64(b), 0.0)

@@ -1,0 +1,54 @@
+import concourse.mybir as mybir
+
+ROWS, PLACES, N, M = 256, 2048, 2048, 128
+P = 128
+BLOCKS = ROWS // P
+PIECE = 512
+FLOPS = 2 * ROWS * M * N
+
+F32, BF16, U16 = mybir.dt.float32, mybir.dt.bfloat16, mybir.dt.uint16
+MAX, MULT = mybir.AluOpType.max, mybir.AluOpType.mult
+SILU, RELU = mybir.ActivationFunctionType.Silu, mybir.ActivationFunctionType.Relu
+
+
+def tile_lookup_vg_maxsilu_relu_kernel(tc, tab, y, w, b, offs, out):
+    nc = tc.nc
+    with (
+        tc.tile_pool(name="held", bufs=1) as held,
+        tc.tile_pool(name="work", bufs=4) as work,
+        tc.psum_pool(name="psum", bufs=1) as psum,
+    ):
+        offsets = held.tile([P, N // 16], U16, name="offsets")
+        nc.sync.dma_start(offsets[:], offs)
+        weights = held.tile([P, BLOCKS, M], BF16, name="weights")
+        nc.gpsimd.dma_start(weights[:], w.rearrange("(k p) m -> p k m", p=P))
+        bias = held.tile([P, 1], F32, name="bias")
+        nc.gpsimd.dma_start(bias[:], b)
+
+        values, gates, stream = [], [], []
+        for k in range(BLOCKS):
+            rows = slice(k * P, (k + 1) * P)
+            values.append(held.tile([P, PLACES], F32, name=f"values{k}"))
+            stream.append(held.tile([P, N], F32, name=f"stream{k}"))
+            gates.append(held.tile([P, PLACES], F32, name=f"gates{k}"))
+            nc.sync.dma_start(values[k][:], tab[0, rows, :])
+            nc.sync.dma_start(stream[k][:], y[rows, :])
+            nc.sync.dma_start(gates[k][:], tab[1, rows, :])
+
+        banks = [psum.tile([P, PIECE], F32, name=f"bank{c}") for c in range(N // PIECE)]
+        for k in range(BLOCKS):
+            for c in range(N // PIECE):
+                cols = slice(c * PIECE, (c + 1) * PIECE)
+                piece = offsets[:, c * PIECE // 16 : (c + 1) * PIECE // 16]
+                larger = work.tile([P, PIECE], F32, name="larger")
+                nc.vector.tensor_tensor(larger[:], values[k][:].indirect(piece), stream[k][:, cols], MAX)
+                gate = work.tile([P, PIECE], F32, name="gate")
+                nc.scalar.activation(gate[:], gates[k][:].indirect(piece), SILU)
+                x = work.tile([P, PIECE], BF16, name="x")
+                nc.vector.tensor_tensor(x[:], larger[:], gate[:], MULT)
+                nc.tensor.matmul(banks[c][:], weights[:, k, :], x[:], start=k == 0, stop=k == BLOCKS - 1)
+
+        for c in range(N // PIECE):
+            result = work.tile([P, PIECE], F32, name="result")
+            nc.scalar.activation(result[:], banks[c][:], RELU, bias=bias[:])
+            nc.sync.dma_start(out[:, c * PIECE : (c + 1) * PIECE], result[:])

@@ -4,6 +4,7 @@ ROWS, PLACES, N, M = 256, 2048, 2048, 128
 P = 128
 BLOCKS = ROWS // P
 PIECE = 512
+PIECES = N // PIECE
 FLOPS = 2 * ROWS * M * N
 
 F32, BF16, U16 = mybir.dt.float32, mybir.dt.bfloat16, mybir.dt.uint16
@@ -18,37 +19,66 @@ def tile_lookup_vg_maxsilu_relu_kernel(tc, tab, y, w, b, offs, out):
         tc.tile_pool(name="work", bufs=4) as work,
         tc.psum_pool(name="psum", bufs=1) as psum,
     ):
+        idle = held.tile([P, 1], F32, name="idle")
+        warmed = held.tile([P, 1], F32, name="warmed")
+        nc.vector.memset(idle[:], 0.0)
+        nc.scalar.activation(warmed[:], idle[:], SILU)
+
         offsets = held.tile([P, N // 16], U16, name="offsets")
         nc.sync.dma_start(offsets[:], offs)
         weights = held.tile([P, BLOCKS, M], BF16, name="weights")
-        nc.gpsimd.dma_start(weights[:], w.rearrange("(k p) m -> p k m", p=P))
+        nc.scalar.dma_start(weights[:], w.rearrange("(k p) m -> p k m", p=P))
         bias = held.tile([P, 1], F32, name="bias")
-        nc.gpsimd.dma_start(bias[:], b)
+        nc.scalar.dma_start(bias[:], b)
 
-        values, gates, stream = [], [], []
+        values = [held.tile([P, PLACES], F32, name=f"values{k}") for k in range(BLOCKS)]
+        gates = [held.tile([P, PLACES], F32, name=f"gates{k}") for k in range(BLOCKS)]
+        stream = [held.tile([P, N], F32, name=f"stream{k}") for k in range(BLOCKS)]
+        larger = [held.tile([P, N], F32, name=f"larger{k}") for k in range(BLOCKS)]
+
+        def load_window(window, table, k):
+            nc.sync.dma_start(window[k][:], tab[table, k * P : (k + 1) * P, :])
+
+        def load_stream(k, c):
+            nc.sync.dma_start(stream[k][:, cols(c)], y[k * P : (k + 1) * P, cols(c)])
+
+        def cols(c):
+            return slice(c * PIECE, (c + 1) * PIECE)
+
+        def piece(c):
+            return offsets[:, c * PIECE // 16 : (c + 1) * PIECE // 16]
+
         for k in range(BLOCKS):
-            rows = slice(k * P, (k + 1) * P)
-            values.append(held.tile([P, PLACES], F32, name=f"values{k}"))
-            stream.append(held.tile([P, N], F32, name=f"stream{k}"))
-            gates.append(held.tile([P, PLACES], F32, name=f"gates{k}"))
-            nc.sync.dma_start(values[k][:], tab[0, rows, :])
-            nc.sync.dma_start(stream[k][:], y[rows, :])
-            nc.sync.dma_start(gates[k][:], tab[1, rows, :])
+            load_window(values, 0, k)
+            for c in range(PIECES // 2):
+                load_stream(k, c)
+            load_window(gates, 1, k)
+            for c in range(PIECES // 2, PIECES):
+                load_stream(k, c)
 
-        banks = [psum.tile([P, PIECE], F32, name=f"bank{c}") for c in range(N // PIECE)]
+        banks = [psum.tile([P, PIECE], F32, name=f"bank{c}") for c in range(PIECES)]
+
+        def maxima(k, c):
+            nc.vector.tensor_tensor(larger[k][:, cols(c)], values[k][:].indirect(piece(c)), stream[k][:, cols(c)], MAX)
+
+        def gate_and_multiply(k, c):
+            gate = work.tile([P, PIECE], F32, name="gate")
+            nc.scalar.activation(gate[:], gates[k][:].indirect(piece(c)), SILU)
+            x = work.tile([P, PIECE], BF16, name="x")
+            nc.vector.tensor_tensor(x[:], larger[k][:, cols(c)], gate[:], MULT)
+            nc.tensor.matmul(banks[c][:], weights[:, k, :], x[:], start=k == 0, stop=k == BLOCKS - 1)
+
+        for c in range(PIECES):
+            maxima(0, c)
         for k in range(BLOCKS):
-            for c in range(N // PIECE):
-                cols = slice(c * PIECE, (c + 1) * PIECE)
-                piece = offsets[:, c * PIECE // 16 : (c + 1) * PIECE // 16]
-                larger = work.tile([P, PIECE], F32, name="larger")
-                nc.vector.tensor_tensor(larger[:], values[k][:].indirect(piece), stream[k][:, cols], MAX)
-                gate = work.tile([P, PIECE], F32, name="gate")
-                nc.scalar.activation(gate[:], gates[k][:].indirect(piece), SILU)
-                x = work.tile([P, PIECE], BF16, name="x")
-                nc.vector.tensor_tensor(x[:], larger[:], gate[:], MULT)
-                nc.tensor.matmul(banks[c][:], weights[:, k, :], x[:], start=k == 0, stop=k == BLOCKS - 1)
+            for pair in range(0, PIECES, 2):
+                for c in (pair, pair + 1):
+                    gate_and_multiply(k, c)
+                if k + 1 < BLOCKS:
+                    for c in (pair, pair + 1):
+                        maxima(k + 1, c)
 
-        for c in range(N // PIECE):
+        for c in range(PIECES):
             result = work.tile([P, PIECE], F32, name="result")
             nc.scalar.activation(result[:], banks[c][:], RELU, bias=bias[:])
-            nc.sync.dma_start(out[:, c * PIECE : (c + 1) * PIECE], result[:])
+            nc.sync.dma_start(out[:, cols(c)], result[:])

@@ -16,7 +16,6 @@ def tile_lookup_vg_maxsilu_relu_kernel(tc, tab, y, w, b, offs, out):
     nc = tc.nc
     with (
         tc.tile_pool(name="held", bufs=1) as held,
-        tc.tile_pool(name="work", bufs=4) as work,
         tc.psum_pool(name="psum", bufs=1) as psum,
     ):
         idle = held.tile([P, 1], F32, name="idle")
@@ -25,60 +24,67 @@ def tile_lookup_vg_maxsilu_relu_kernel(tc, tab, y, w, b, offs, out):
         nc.scalar.activation(warmed[:], idle[:], SILU)
 
         offsets = held.tile([P, N // 16], U16, name="offsets")
-        nc.sync.dma_start(offsets[:], offs)
         weights = held.tile([P, BLOCKS, M], BF16, name="weights")
-        nc.scalar.dma_start(weights[:], w.rearrange("(k p) m -> p k m", p=P))
         bias = held.tile([P, 1], F32, name="bias")
-        nc.scalar.dma_start(bias[:], b)
 
-        values = [held.tile([P, PLACES], F32, name=f"values{k}") for k in range(BLOCKS)]
-        gates = [held.tile([P, PLACES], F32, name=f"gates{k}") for k in range(BLOCKS)]
-        stream = [held.tile([P, N], F32, name=f"stream{k}") for k in range(BLOCKS)]
-        larger = [held.tile([P, N], F32, name=f"larger{k}") for k in range(BLOCKS)]
+        def block_tiles(name, dtype):
+            return [held.tile([P, N], dtype, name=f"{name}{k}") for k in range(BLOCKS)]
+
+        values, gates, stream = block_tiles("values", F32), block_tiles("gates", F32), block_tiles("stream", F32)
+        larger, opened, x = block_tiles("larger", F32), block_tiles("opened", F32), block_tiles("x", BF16)
+        result = held.tile([P, N], F32, name="result")
+
+        pieces = [slice(at, at + PIECE) for at in range(0, N, PIECE)]
+        parts = pieces[:-1] + [slice(N - PIECE, N - PIECE // 2), slice(N - PIECE // 2, N)]
+        banks = [psum.tile([P, PIECE], F32, name=f"bank{i}") for i in range(len(parts))]
 
         def load_window(window, table, k):
             nc.sync.dma_start(window[k][:], tab[table, k * P : (k + 1) * P, :])
 
-        def load_stream(k, c):
-            nc.sync.dma_start(stream[k][:, cols(c)], y[k * P : (k + 1) * P, cols(c)])
+        def load_stream(k, cols):
+            nc.sync.dma_start(stream[k][:, cols], y[k * P : (k + 1) * P, cols])
 
-        def cols(c):
-            return slice(c * PIECE, (c + 1) * PIECE)
+        def places(cols):
+            return offsets[:, cols.start // 16 : cols.stop // 16]
 
-        def piece(c):
-            return offsets[:, c * PIECE // 16 : (c + 1) * PIECE // 16]
+        def look_up_value(k, cols):
+            nc.vector.tensor_tensor(larger[k][:, cols], values[k][:].indirect(places(cols)), stream[k][:, cols], MAX)
 
+        def look_up_gate(k, cols):
+            nc.scalar.activation(opened[k][:, cols], gates[k][:].indirect(places(cols)), SILU)
+
+        def multiply(k, i):
+            cols = parts[i]
+            nc.vector.tensor_tensor(x[k][:, cols], larger[k][:, cols], opened[k][:, cols], MULT)
+            width = cols.stop - cols.start
+            nc.tensor.matmul(banks[i][:, :width], weights[:, k, :], x[k][:, cols], start=k == 0, stop=k == BLOCKS - 1)
+
+        nc.sync.dma_start(offsets[:], offs)
         for k in range(BLOCKS):
             load_window(values, 0, k)
-            for c in range(PIECES // 2):
-                load_stream(k, c)
+            for cols in pieces[:2]:
+                load_stream(k, cols)
             load_window(gates, 1, k)
-            for c in range(PIECES // 2, PIECES):
-                load_stream(k, c)
+            for cols in pieces[2:]:
+                load_stream(k, cols)
+            if k == 0:
+                nc.sync.dma_start(weights[:], w.rearrange("(k p) m -> p k m", p=P))
+                nc.sync.dma_start(bias[:], b)
 
-        banks = [psum.tile([P, PIECE], F32, name=f"bank{c}") for c in range(PIECES)]
-
-        def maxima(k, c):
-            nc.vector.tensor_tensor(larger[k][:, cols(c)], values[k][:].indirect(piece(c)), stream[k][:, cols(c)], MAX)
-
-        def gate_and_multiply(k, c):
-            gate = work.tile([P, PIECE], F32, name="gate")
-            nc.scalar.activation(gate[:], gates[k][:].indirect(piece(c)), SILU)
-            x = work.tile([P, PIECE], BF16, name="x")
-            nc.vector.tensor_tensor(x[:], larger[k][:, cols(c)], gate[:], MULT)
-            nc.tensor.matmul(banks[c][:], weights[:, k, :], x[:], start=k == 0, stop=k == BLOCKS - 1)
-
-        for c in range(PIECES):
-            maxima(0, c)
+        for cols in pieces:
+            look_up_value(0, cols)
         for k in range(BLOCKS):
-            for pair in range(0, PIECES, 2):
-                for c in (pair, pair + 1):
-                    gate_and_multiply(k, c)
+            for pair in (0, 1):
+                mine = slice(2 * pair, 2 * pair + 2)
+                for cols in pieces[mine]:
+                    look_up_gate(k, cols)
+                for i in ((0, 1), range(2, len(parts)))[pair]:
+                    multiply(k, i)
                 if k + 1 < BLOCKS:
-                    for c in (pair, pair + 1):
-                        maxima(k + 1, c)
+                    for cols in pieces[mine]:
+                        look_up_value(k + 1, cols)
 
-        for c in range(PIECES):
-            result = work.tile([P, PIECE], F32, name="result")
-            nc.scalar.activation(result[:], banks[c][:], RELU, bias=bias[:])
-            nc.sync.dma_start(out[:, cols(c)], result[:])
+        for i in range(len(parts)):
+            cols = parts[i]
+            nc.scalar.activation(result[:, cols], banks[i][:, : cols.stop - cols.start], RELU, bias=bias[:])
+            nc.sync.dma_start(out[:, cols], result[:, cols])

@@ -67,9 +67,8 @@ def tile_lookup_vg_maxsilu_relu_kernel(tc, tab, y, w, b, offs, out):
             load_window(gates, 1, k)
             for cols in pieces[2:]:
                 load_stream(k, cols)
-            if k == 0:
-                nc.sync.dma_start(weights[:], w.rearrange("(k p) m -> p k m", p=P))
-                nc.sync.dma_start(bias[:], b)
+        nc.sync.dma_start(weights[:], w.rearrange("(k p) m -> p k m", p=P))
+        nc.sync.dma_start(bias[:], b)
 
         for cols in pieces:
             look_up_value(0, cols)

import concourse.mybir as mybir

ROWS, PLACES, N, M = 256, 2048, 2048, 128
P = 128
BLOCKS = ROWS // P
PIECE = 512
PIECES = N // PIECE
FLOPS = 2 * ROWS * M * N

F32, BF16, U16 = mybir.dt.float32, mybir.dt.bfloat16, mybir.dt.uint16
MAX, MULT = mybir.AluOpType.max, mybir.AluOpType.mult
SILU, RELU = mybir.ActivationFunctionType.Silu, mybir.ActivationFunctionType.Relu


def tile_lookup_vg_maxsilu_relu_kernel(tc, tab, y, w, b, offs, out):
    nc = tc.nc
    with (
        tc.tile_pool(name="held", bufs=1) as held,
        tc.psum_pool(name="psum", bufs=1) as psum,
    ):
        idle = held.tile([P, 1], F32, name="idle")
        warmed = held.tile([P, 1], F32, name="warmed")
        nc.vector.memset(idle[:], 0.0)
        nc.scalar.activation(warmed[:], idle[:], SILU)

        offsets = held.tile([P, N // 16], U16, name="offsets")
        weights = held.tile([P, BLOCKS, M], BF16, name="weights")
        bias = held.tile([P, 1], F32, name="bias")

        def block_tiles(name, dtype):
            return [held.tile([P, N], dtype, name=f"{name}{k}") for k in range(BLOCKS)]

        values, gates, stream = block_tiles("values", F32), block_tiles("gates", F32), block_tiles("stream", F32)
        larger, opened, x = block_tiles("larger", F32), block_tiles("opened", F32), block_tiles("x", BF16)
        result = held.tile([P, N], F32, name="result")

        pieces = [slice(at, at + PIECE) for at in range(0, N, PIECE)]
        parts = pieces[:-1] + [slice(N - PIECE, N - PIECE // 2), slice(N - PIECE // 2, N)]
        banks = [psum.tile([P, PIECE], F32, name=f"bank{i}") for i in range(len(parts))]

        def load_window(window, table, k):
            nc.sync.dma_start(window[k][:], tab[table, k * P : (k + 1) * P, :])

        def load_stream(k, cols):
            nc.sync.dma_start(stream[k][:, cols], y[k * P : (k + 1) * P, cols])

        def places(cols):
            return offsets[:, cols.start // 16 : cols.stop // 16]

        def look_up_value(k, cols):
            nc.vector.tensor_tensor(larger[k][:, cols], values[k][:].indirect(places(cols)), stream[k][:, cols], MAX)

        def look_up_gate(k, cols):
            nc.scalar.activation(opened[k][:, cols], gates[k][:].indirect(places(cols)), SILU)

        def multiply(k, i):
            cols = parts[i]
            nc.vector.tensor_tensor(x[k][:, cols], larger[k][:, cols], opened[k][:, cols], MULT)
            width = cols.stop - cols.start
            nc.tensor.matmul(banks[i][:, :width], weights[:, k, :], x[k][:, cols], start=k == 0, stop=k == BLOCKS - 1)

        nc.sync.dma_start(offsets[:], offs)
        for k in range(BLOCKS):
            load_window(values, 0, k)
            for cols in pieces[:2]:
                load_stream(k, cols)
            load_window(gates, 1, k)
            for cols in pieces[2:]:
                load_stream(k, cols)
        nc.sync.dma_start(weights[:], w.rearrange("(k p) m -> p k m", p=P))
        nc.sync.dma_start(bias[:], b)

        for cols in pieces:
            look_up_value(0, cols)
        for k in range(BLOCKS):
            for pair in (0, 1):
                mine = slice(2 * pair, 2 * pair + 2)
                for cols in pieces[mine]:
                    look_up_gate(k, cols)
                for i in ((0, 1), range(2, len(parts)))[pair]:
                    multiply(k, i)
                if k + 1 < BLOCKS:
                    for cols in pieces[mine]:
                        look_up_value(k + 1, cols)

        for i in range(len(parts)):
            cols = parts[i]
            nc.scalar.activation(result[:, cols], banks[i][:, : cols.stop - cols.start], RELU, bias=bias[:])
            nc.sync.dma_start(out[:, cols], result[:, cols])
